import numpy as np
import ml_dtypes


def mxq(x, axis, fmt="e4m3"):
    dtype, down = {"e4m3": (ml_dtypes.float8_e4m3fn, 7), "e5m2": (ml_dtypes.float8_e5m2, 14)}[fmt]
    v = np.moveaxis(np.asarray(x, np.float32).astype(ml_dtypes.bfloat16).astype(np.float64), axis, -1)
    blocks = v.reshape(v.shape[:-1] + (-1, 32))
    amax = np.abs(blocks).max(-1, keepdims=True)
    byte = np.maximum(np.where(amax > 0, np.frexp(amax)[1] - 1 + 127, 0) - down, 1)
    scale = np.exp2(byte - 127.0)
    codes = (blocks / scale).astype(np.float32).astype(dtype).astype(np.float64)
    return np.moveaxis((codes * scale).reshape(v.shape), -1, axis)


WIDE = False


def mx_kscale(k):
    if not WIDE:
        return np.ones(k)
    levels = np.array([10, -10, 5, -5, 0])
    if k % 512:
        return np.exp2(np.random.permutation(np.resize(levels, k // 32))).repeat(32)
    a = np.empty((k // 512, 16))
    for p in range(k // 512):
        a[p, :8] = np.random.permutation(np.resize(levels, 8))
        for g in range(8):
            far = levels[np.abs(levels - a[p, g]) >= 10]
            a[p, g + 8] = far[np.random.randint(len(far))]
    return np.exp2(a.ravel()).repeat(32)


def f64(x):
    return np.asarray(x).astype(np.float64)


def striped(idx):
    return np.tile(idx.reshape(-1, 16).T, (8, 1)).astype(np.uint16)


def unstriped(offs):
    return offs[:16].T.reshape(-1).astype(np.int64)


def striped8(idx):
    return np.concatenate([x.reshape(-1, 16).T for x in idx]).astype(np.uint16)


def runs(offs, k):
    lists = np.stack([offs[16 * r : 16 * r + 16].T.reshape(-1) for r in range(8)]).astype(np.int64)
    return lists[np.arange(k) % 512 // 64]


def pack_weight(w):
    k, n = w.shape
    w = f64(np.asarray(w, np.float32).astype(ml_dtypes.bfloat16)).reshape(k // 32, 32, n)
    amax = np.abs(w).max(1)
    byte = np.clip(np.where(amax > 0, np.frexp(amax)[1] - 1 + 127 - 7, 1), 1, 254)
    scaled = (w * np.exp2(127.0 - byte)[:, None, :]).reshape(k, n).astype(np.float32)
    words = np.ascontiguousarray(scaled.reshape(k // 512, 128, 4, n).transpose(0, 1, 3, 2)).astype(ml_dtypes.float8_e4m3fn).view(np.uint8)
    return words, np.ascontiguousarray(byte.astype(np.uint8).reshape(k // 512, 16, n))


def unpack_weight(words, scales):
    g, p, n, _ = words.shape
    vals = np.ascontiguousarray(words).view(ml_dtypes.float8_e4m3fn).astype(np.float64) * np.repeat(np.exp2(scales.astype(np.float64) - 127.0), 8, axis=1)[..., None]
    return vals.transpose(0, 1, 3, 2).reshape(g * 512, n)


K, T, S, N, U = 512, 2048, 512, 256, 2048


def setup_inputs():
    n = np.random.standard_normal
    s = mx_kscale(K)[:, None]
    packed_xT = pack_weight(n((K, T)) * s)
    return {
        "x_words": packed_xT[0],
        "x_scales": packed_xT[1],
        "mem": n((N, U)).astype(np.float32),
        "w1": (n((K, N)) / np.sqrt(K) / s).astype(np.float32),
        "offs": striped8(np.stack([np.random.permutation(T)[:S] for _ in range(8)])),
        "slot": striped(np.random.permutation(U)[:S]),
    }


def reference(x_words, x_scales, mem, w1, offs, slot):
    xq = unpack_weight(x_words, x_scales)[np.arange(K)[:, None], runs(offs, K)]
    y = mxq(f64(w1), 0, "e4m3").T @ xq
    out = f64(mem).copy()
    out[:, unstriped(slot)] = y
    return out

@@ -1,0 +1,92 @@
+from contextlib import ExitStack
+
+import concourse.mybir as mybir
+
+K, T, S, N, U = 512, 2048, 512, 256, 2048
+FLOPS = 2 * K * N * S
+
+F32 = mybir.dt.float32
+BF16 = mybir.dt.bfloat16
+I32 = mybir.dt.int32
+U32 = mybir.dt.uint32
+U16 = mybir.dt.uint16
+U8 = mybir.dt.uint8
+FP8X4 = mybir.dt.float8_e4m3fn_x4
+
+P = 128
+PACK = 4
+HALF = S // 2
+
+
+def tile_picked_phput_none_p_kernel(tc, x_words, x_scales, mem, w1, offs, slot, out):
+    nc = tc.nc
+    with ExitStack() as ctx:
+        keep = ctx.enter_context(tc.tile_pool(name="keep", bufs=1))
+        psum = ctx.enter_context(tc.psum_pool(name="psum", bufs=1))
+
+        offs_sb = keep.tile([P, S // 16], U16, name="offs_sb")
+        nc.sync.dma_start(offs_sb[:], offs)
+
+        scale_table = keep.tile([P, T], U8, name="scale_table", align_bytes=64)
+        nc.vector.memset(scale_table[:].bitcast(I32), 0)
+        nc.sync.dma_start(scale_table[0:P:8, :].bitcast(I32), x_scales[0].bitcast(I32))
+
+        slot_sb = keep.tile([P, S // 16], U16, name="slot_sb")
+        nc.sync.dma_start(slot_sb[:], slot)
+
+        w_raw = keep.tile([P, PACK, N], F32, name="w_raw")
+        nc.scalar.dma_start(w_raw[:], w1.rearrange("(p j) n -> p j n", j=PACK))
+        word_table = keep.tile([P, T], I32, name="word_table", align_bytes=64)
+        nc.scalar.dma_start(word_table[:], x_words[0].rearrange("p n t -> p (n t)").bitcast(I32))
+        windows = []
+        for b in range(N // P):
+            window = keep.tile([P, U], F32, name="window%d" % b)
+            nc.scalar.dma_start(window[:], mem[b * P : (b + 1) * P, :])
+            windows.append(window)
+
+        x_plane = keep.tile([P, S], U8, name="x_plane", align_bytes=64)
+        nc.vector.memset(x_plane[:].bitcast(I32), 0)
+
+        picked_scales = keep.tile([P, S], U8, name="picked_scales", align_bytes=64)
+        nc.vector.tensor_copy(picked_scales[:], scale_table[:].indirect(offs_sb[:]))
+        for q in range(4):
+            nc.sync.dma_start(
+                x_plane[32 * q : 32 * q + 4, :].bitcast(I32),
+                picked_scales[32 * q : 32 * (q + 1) : 8, :].bitcast(I32),
+            )
+
+        w_grouped = keep.tile([P, N, PACK], BF16, name="w_grouped", align_bytes=64)
+        nc.scalar.copy(w_grouped[:], w_raw[:].rearrange("p j n -> p n j"))
+        w_codes = keep.tile([P, N], U32, name="w_codes", align_bytes=64)
+        w_plane = keep.tile([P, N], U8, name="w_plane", align_bytes=64)
+        nc.vector.quantize_mx(
+            out=w_codes[:].bitcast(FP8X4),
+            scales=w_plane[:],
+            in_=w_grouped[:].rearrange("p n j -> p (n j)"),
+        )
+
+        picked = []
+        for h in range(2):
+            picked_words = keep.tile([P, HALF], U32, name="picked_words%d" % h, align_bytes=64)
+            entries = offs_sb[:, h * HALF // 16 : (h + 1) * HALF // 16]
+            nc.vector.tensor_copy(picked_words[:], word_table[:].bitcast(U32).indirect(entries))
+            picked.append(picked_words)
+
+        for b in range(N // P):
+            rows = slice(b * P, (b + 1) * P)
+            y = keep.tile([P, S], F32, name="y%d" % b)
+            for h in range(2):
+                cols = slice(h * HALF, (h + 1) * HALF)
+                acc = psum.tile([P, HALF], F32, name="acc%d%d" % (b, h))
+                nc.tensor.matmul_mx(
+                    out=acc[:],
+                    lhsT=w_codes[:, rows].bitcast(FP8X4),
+                    lhsT_scale=w_plane[:, rows],
+                    rhs=picked[h][:].bitcast(FP8X4),
+                    rhs_scale=x_plane[:, cols],
+                    start=True,
+                    stop=True,
+                )
+                nc.scalar.copy(y[:, cols], acc[:])
+            nc.vector.tensor_copy(windows[b][:].indirect(slot_sb[:]), y[:])
+            nc.sync.dma_start(out[rows, :], windows[b][:])

@@ -16,6 +16,7 @@ FP8X4 = mybir.dt.float8_e4m3fn_x4
 P = 128
 PACK = 4
 HALF = S // 2
+STAGE = U - PACK * N
 
 
 def tile_picked_phput_none_p_kernel(tc, x_words, x_scales, mem, w1, offs, slot, out):
@@ -24,28 +25,31 @@ def tile_picked_phput_none_p_kernel(tc, x_words, x_scales, mem, w1, offs, slot, 
         keep = ctx.enter_context(tc.tile_pool(name="keep", bufs=1))
         psum = ctx.enter_context(tc.psum_pool(name="psum", bufs=1))
 
-        offs_sb = keep.tile([P, S // 16], U16, name="offs_sb")
-        nc.sync.dma_start(offs_sb[:], offs)
-
         scale_table = keep.tile([P, T], U8, name="scale_table", align_bytes=64)
         nc.vector.memset(scale_table[:].bitcast(I32), 0)
-        nc.sync.dma_start(scale_table[0:P:8, :].bitcast(I32), x_scales[0].bitcast(I32))
 
+        window0 = keep.tile([P, U], F32, name="window0", align_bytes=64)
+        w_raw = window0[:, STAGE:U].rearrange("p (j n) -> p j n", j=PACK)
+        w_rows = w1.rearrange("(p j) n -> p j n", j=PACK)
+
+        offs_sb = keep.tile([P, S // 16], U16, name="offs_sb")
+        nc.sync.dma_start(offs_sb[:], offs)
+        nc.sync.dma_start(w_raw[:, 0:2, :], w_rows[:, 0:2, :])
         slot_sb = keep.tile([P, S // 16], U16, name="slot_sb")
         nc.sync.dma_start(slot_sb[:], slot)
-
-        w_raw = keep.tile([P, PACK, N], F32, name="w_raw")
-        nc.scalar.dma_start(w_raw[:], w1.rearrange("(p j) n -> p j n", j=PACK))
+        nc.sync.dma_start(scale_table[0:P:8, :].bitcast(I32), x_scales[0].bitcast(I32))
+        nc.sync.dma_start(w_raw[:, 2:4, :], w_rows[:, 2:4, :])
         word_table = keep.tile([P, T], I32, name="word_table", align_bytes=64)
-        nc.scalar.dma_start(word_table[:], x_words[0].rearrange("p n t -> p (n t)").bitcast(I32))
-        windows = []
-        for b in range(N // P):
-            window = keep.tile([P, U], F32, name="window%d" % b)
-            nc.scalar.dma_start(window[:], mem[b * P : (b + 1) * P, :])
-            windows.append(window)
+        nc.sync.dma_start(word_table[:], x_words[0].rearrange("p n t -> p (n t)").bitcast(I32))
+        nc.sync.dma_start(window0[:, 0:STAGE], mem[0:P, 0:STAGE])
 
         x_plane = keep.tile([P, S], U8, name="x_plane", align_bytes=64)
         nc.vector.memset(x_plane[:].bitcast(I32), 0)
+
+        warm_in = keep.tile([P, 1], F32, name="warm_in")
+        nc.vector.memset(warm_in[:], 0.0)
+        warm_out = keep.tile([P, 1], F32, name="warm_out")
+        nc.scalar.copy(warm_out[:], warm_in[:])
 
         picked_scales = keep.tile([P, S], U8, name="picked_scales", align_bytes=64)
         nc.vector.tensor_copy(picked_scales[:], scale_table[:].indirect(offs_sb[:]))
@@ -55,8 +59,9 @@ def tile_picked_phput_none_p_kernel(tc, x_words, x_scales, mem, w1, offs, slot, 
                 picked_scales[32 * q : 32 * (q + 1) : 8, :].bitcast(I32),
             )
 
-        w_grouped = keep.tile([P, N, PACK], BF16, name="w_grouped", align_bytes=64)
-        nc.scalar.copy(w_grouped[:], w_raw[:].rearrange("p j n -> p n j"))
+        w_grouped = keep.tile([P, N, PACK], BF16, name="w_grouped", tag="second", align_bytes=64)
+        nc.scalar.copy(w_grouped[:], w_raw.rearrange("p j n -> p n j"))
+        nc.sync.dma_start(window0[:, STAGE:U], mem[0:P, STAGE:U])
         w_codes = keep.tile([P, N], U32, name="w_codes", align_bytes=64)
         w_plane = keep.tile([P, N], U8, name="w_plane", align_bytes=64)
         nc.vector.quantize_mx(
@@ -64,6 +69,9 @@ def tile_picked_phput_none_p_kernel(tc, x_words, x_scales, mem, w1, offs, slot, 
             scales=w_plane[:],
             in_=w_grouped[:].rearrange("p n j -> p (n j)"),
         )
+        window1 = keep.tile([P, U], F32, name="window1", tag="second", align_bytes=64)
+        nc.sync.dma_start(window1[:], mem[P : 2 * P, :])
+        windows = [window0, window1]
 
         picked = []
         for h in range(2):

@@ -17,6 +17,7 @@ P = 128
 PACK = 4
 HALF = S // 2
 STAGE = U - PACK * N
+EARLY = 768
 
 
 def tile_picked_phput_none_p_kernel(tc, x_words, x_scales, mem, w1, offs, slot, out):
@@ -41,7 +42,7 @@ def tile_picked_phput_none_p_kernel(tc, x_words, x_scales, mem, w1, offs, slot, 
         nc.sync.dma_start(w_raw[:, 2:4, :], w_rows[:, 2:4, :])
         word_table = keep.tile([P, T], I32, name="word_table", align_bytes=64)
         nc.sync.dma_start(word_table[:], x_words[0].rearrange("p n t -> p (n t)").bitcast(I32))
-        nc.sync.dma_start(window0[:, 0:STAGE], mem[0:P, 0:STAGE])
+        nc.sync.dma_start(window0[:, 0:EARLY], mem[0:P, 0:EARLY])
 
         x_plane = keep.tile([P, S], U8, name="x_plane", align_bytes=64)
         nc.vector.memset(x_plane[:].bitcast(I32), 0)
@@ -60,8 +61,11 @@ def tile_picked_phput_none_p_kernel(tc, x_words, x_scales, mem, w1, offs, slot, 
             )
 
         w_grouped = keep.tile([P, N, PACK], BF16, name="w_grouped", tag="second", align_bytes=64)
-        nc.scalar.copy(w_grouped[:], w_raw.rearrange("p j n -> p n j"))
-        nc.sync.dma_start(window0[:, STAGE:U], mem[0:P, STAGE:U])
+        nc.scalar.copy(
+            w_grouped[:].rearrange("p (c i) j -> p c j i", i=4),
+            w_raw.rearrange("p j (c i) -> p c j i", i=4),
+        )
+        nc.sync.dma_start(window0[:, EARLY:U], mem[0:P, EARLY:U])
         w_codes = keep.tile([P, N], U32, name="w_codes", align_bytes=64)
         w_plane = keep.tile([P, N], U8, name="w_plane", align_bytes=64)
         nc.vector.quantize_mx(

@@ -34,8 +34,8 @@ def tile_picked_phput_none_p_kernel(tc, x_words, x_scales, mem, w1, offs, slot, 
         w_rows = w1.rearrange("(p j) n -> p j n", j=PACK)
 
         offs_sb = keep.tile([P, S // 16], U16, name="offs_sb")
-        nc.sync.dma_start(offs_sb[:], offs)
         nc.sync.dma_start(w_raw[:, 0:2, :], w_rows[:, 0:2, :])
+        nc.sync.dma_start(offs_sb[:], offs)
         slot_sb = keep.tile([P, S // 16], U16, name="slot_sb")
         nc.sync.dma_start(slot_sb[:], slot)
         nc.sync.dma_start(scale_table[0:P:8, :].bitcast(I32), x_scales[0].bitcast(I32))
@@ -101,4 +101,8 @@ def tile_picked_phput_none_p_kernel(tc, x_words, x_scales, mem, w1, offs, slot, 
                 )
                 nc.scalar.copy(y[:, cols], acc[:])
             nc.vector.tensor_copy(windows[b][:].indirect(slot_sb[:]), y[:])
-            nc.sync.dma_start(out[rows, :], windows[b][:])
+            if b == 0:
+                nc.sync.dma_start(out[rows, :], windows[b][:])
+            else:
+                nc.sync.dma_start(out[rows, 0 : U // 2], windows[b][:, 0 : U // 2])
+                nc.scalar.dma_start(out[rows, U // 2 : U], windows[b][:, U // 2 : U])

@@ -16,8 +16,8 @@ FP8X4 = mybir.dt.float8_e4m3fn_x4
 P = 128
 PACK = 4
 HALF = S // 2
-STAGE = U - PACK * N
-EARLY = 768
+STAGE = U - P * PACK // 2
+EARLY = 704
 
 
 def tile_picked_phput_none_p_kernel(tc, x_words, x_scales, mem, w1, offs, slot, out):
@@ -26,22 +26,23 @@ def tile_picked_phput_none_p_kernel(tc, x_words, x_scales, mem, w1, offs, slot, 
         keep = ctx.enter_context(tc.tile_pool(name="keep", bufs=1))
         psum = ctx.enter_context(tc.psum_pool(name="psum", bufs=1))
 
-        scale_table = keep.tile([P, T], U8, name="scale_table", align_bytes=64)
+        scale_table = keep.tile([P, T], U8, name="scale_table", tag="table", align_bytes=64)
         nc.vector.memset(scale_table[:].bitcast(I32), 0)
 
         window0 = keep.tile([P, U], F32, name="window0", align_bytes=64)
-        w_raw = window0[:, STAGE:U].rearrange("p (j n) -> p j n", j=PACK)
         w_rows = w1.rearrange("(p j) n -> p j n", j=PACK)
+        w_raw0 = keep.tile([P, PACK, P], F32, name="w_raw0", align_bytes=64)
+        w_raw1 = keep.tile([P, PACK, P], F32, name="w_raw1", tag="second", align_bytes=64)
 
+        nc.sync.dma_start(w_raw0[:], w_rows[:, :, 0:P])
         offs_sb = keep.tile([P, S // 16], U16, name="offs_sb")
-        nc.sync.dma_start(w_raw[:, 0:2, :], w_rows[:, 0:2, :])
         nc.sync.dma_start(offs_sb[:], offs)
         slot_sb = keep.tile([P, S // 16], U16, name="slot_sb")
         nc.sync.dma_start(slot_sb[:], slot)
         nc.sync.dma_start(scale_table[0:P:8, :].bitcast(I32), x_scales[0].bitcast(I32))
-        nc.sync.dma_start(w_raw[:, 2:4, :], w_rows[:, 2:4, :])
         word_table = keep.tile([P, T], I32, name="word_table", align_bytes=64)
         nc.sync.dma_start(word_table[:], x_words[0].rearrange("p n t -> p (n t)").bitcast(I32))
+        nc.sync.dma_start(w_raw1[:], w_rows[:, :, P : 2 * P])
         nc.sync.dma_start(window0[:, 0:EARLY], mem[0:P, 0:EARLY])
 
         x_plane = keep.tile([P, S], U8, name="x_plane", align_bytes=64)
@@ -55,27 +56,27 @@ def tile_picked_phput_none_p_kernel(tc, x_words, x_scales, mem, w1, offs, slot, 
         picked_scales = keep.tile([P, S], U8, name="picked_scales", align_bytes=64)
         nc.vector.tensor_copy(picked_scales[:], scale_table[:].indirect(offs_sb[:]))
         for q in range(4):
-            nc.sync.dma_start(
+            (nc.sync, nc.scalar)[q % 2].dma_start(
                 x_plane[32 * q : 32 * q + 4, :].bitcast(I32),
                 picked_scales[32 * q : 32 * (q + 1) : 8, :].bitcast(I32),
             )
 
-        w_grouped = keep.tile([P, N, PACK], BF16, name="w_grouped", tag="second", align_bytes=64)
-        nc.scalar.copy(
-            w_grouped[:].rearrange("p (c i) j -> p c j i", i=4),
-            w_raw.rearrange("p j (c i) -> p c j i", i=4),
-        )
+        def cast(grouped, raw):
+            nc.scalar.copy(
+                grouped.rearrange("p (c i j) -> p c j i", i=4, j=PACK),
+                raw[:].rearrange("p j (c i) -> p c j i", i=4),
+            )
+
+        def quantise(b, grouped):
+            codes = keep.tile([P, P], U32, name="w_codes%d" % b, align_bytes=64)
+            plane = keep.tile([P, P], U8, name="w_plane%d" % b, tag=("table", "plane1")[b], align_bytes=64)
+            nc.vector.quantize_mx(out=codes[:].bitcast(FP8X4), scales=plane[:], in_=grouped)
+            return codes, plane
+
+        grouped0 = window0[:, STAGE:U].bitcast(BF16)
+        cast(grouped0, w_raw0)
+        weights = [quantise(0, grouped0)]
         nc.sync.dma_start(window0[:, EARLY:U], mem[0:P, EARLY:U])
-        w_codes = keep.tile([P, N], U32, name="w_codes", align_bytes=64)
-        w_plane = keep.tile([P, N], U8, name="w_plane", align_bytes=64)
-        nc.vector.quantize_mx(
-            out=w_codes[:].bitcast(FP8X4),
-            scales=w_plane[:],
-            in_=w_grouped[:].rearrange("p n j -> p (n j)"),
-        )
-        window1 = keep.tile([P, U], F32, name="window1", tag="second", align_bytes=64)
-        nc.sync.dma_start(window1[:], mem[P : 2 * P, :])
-        windows = [window0, window1]
 
         picked = []
         for h in range(2):
@@ -83,6 +84,13 @@ def tile_picked_phput_none_p_kernel(tc, x_words, x_scales, mem, w1, offs, slot, 
             entries = offs_sb[:, h * HALF // 16 : (h + 1) * HALF // 16]
             nc.vector.tensor_copy(picked_words[:], word_table[:].bitcast(U32).indirect(entries))
             picked.append(picked_words)
+
+        grouped1 = keep.tile([P, P * PACK], BF16, name="grouped1", align_bytes=64)
+        cast(grouped1[:], w_raw1)
+        weights.append(quantise(1, grouped1[:]))
+        window1 = keep.tile([P, U], F32, name="window1", tag="second", align_bytes=64)
+        nc.sync.dma_start(window1[:], mem[P : 2 * P, :])
+        windows = [window0, window1]
 
         for b in range(N // P):
             rows = slice(b * P, (b + 1) * P)
@@ -92,8 +100,8 @@ def tile_picked_phput_none_p_kernel(tc, x_words, x_scales, mem, w1, offs, slot, 
                 acc = psum.tile([P, HALF], F32, name="acc%d%d" % (b, h))
                 nc.tensor.matmul_mx(
                     out=acc[:],
-                    lhsT=w_codes[:, rows].bitcast(FP8X4),
-                    lhsT_scale=w_plane[:, rows],
+                    lhsT=weights[b][0][:].bitcast(FP8X4),
+                    lhsT_scale=weights[b][1][:],
                     rhs=picked[h][:].bitcast(FP8X4),
                     rhs_scale=x_plane[:, cols],
                     start=True,

@@ -48,11 +48,6 @@ def tile_picked_phput_none_p_kernel(tc, x_words, x_scales, mem, w1, offs, slot, 
         x_plane = keep.tile([P, S], U8, name="x_plane", align_bytes=64)
         nc.vector.memset(x_plane[:].bitcast(I32), 0)
 
-        warm_in = keep.tile([P, 1], F32, name="warm_in")
-        nc.vector.memset(warm_in[:], 0.0)
-        warm_out = keep.tile([P, 1], F32, name="warm_out")
-        nc.scalar.copy(warm_out[:], warm_in[:])
-
         picked_scales = keep.tile([P, S], U8, name="picked_scales", align_bytes=64)
         nc.vector.tensor_copy(picked_scales[:], scale_table[:].indirect(offs_sb[:]))
         for q in range(4):

@@ -16,25 +16,27 @@ FP8X4 = mybir.dt.float8_e4m3fn_x4
 P = 128
 PACK = 4
 HALF = S // 2
-STAGE = U - P * PACK // 2
-EARLY = 704
+STAGE = U - P * PACK
+EARLY = 1024
+LATE = 32
 
 
 def tile_picked_phput_none_p_kernel(tc, x_words, x_scales, mem, w1, offs, slot, out):
     nc = tc.nc
     with ExitStack() as ctx:
         keep = ctx.enter_context(tc.tile_pool(name="keep", bufs=1))
+        laid = ctx.enter_context(tc.tile_pool(name="laid", bufs=1))
         psum = ctx.enter_context(tc.psum_pool(name="psum", bufs=1))
 
         scale_table = keep.tile([P, T], U8, name="scale_table", tag="table", align_bytes=64)
-        nc.vector.memset(scale_table[:].bitcast(I32), 0)
+        nc.vector.memset(scale_table[:, 0 : T // 2].bitcast(I32), 0)
+        nc.gpsimd.memset(scale_table[:, T // 2 : T].bitcast(I32), 0)
 
         window0 = keep.tile([P, U], F32, name="window0", align_bytes=64)
         w_rows = w1.rearrange("(p j) n -> p j n", j=PACK)
-        w_raw0 = keep.tile([P, PACK, P], F32, name="w_raw0", align_bytes=64)
-        w_raw1 = keep.tile([P, PACK, P], F32, name="w_raw1", tag="second", align_bytes=64)
+        w_raw0 = window0[:, STAGE:U].rearrange("p (j n) -> p j n", j=PACK)
 
-        nc.sync.dma_start(w_raw0[:], w_rows[:, :, 0:P])
+        nc.sync.dma_start(w_raw0, w_rows[:, :, 0:P])
         offs_sb = keep.tile([P, S // 16], U16, name="offs_sb")
         nc.sync.dma_start(offs_sb[:], offs)
         slot_sb = keep.tile([P, S // 16], U16, name="slot_sb")
@@ -42,7 +44,6 @@ def tile_picked_phput_none_p_kernel(tc, x_words, x_scales, mem, w1, offs, slot, 
         nc.sync.dma_start(scale_table[0:P:8, :].bitcast(I32), x_scales[0].bitcast(I32))
         word_table = keep.tile([P, T], I32, name="word_table", align_bytes=64)
         nc.sync.dma_start(word_table[:], x_words[0].rearrange("p n t -> p (n t)").bitcast(I32))
-        nc.sync.dma_start(w_raw1[:], w_rows[:, :, P : 2 * P])
         nc.sync.dma_start(window0[:, 0:EARLY], mem[0:P, 0:EARLY])
 
         x_plane = keep.tile([P, S], U8, name="x_plane", align_bytes=64)
@@ -59,7 +60,7 @@ def tile_picked_phput_none_p_kernel(tc, x_words, x_scales, mem, w1, offs, slot, 
         def cast(grouped, raw):
             nc.scalar.copy(
                 grouped.rearrange("p (c i j) -> p c j i", i=4, j=PACK),
-                raw[:].rearrange("p j (c i) -> p c j i", i=4),
+                raw.rearrange("p j (c i) -> p c j i", i=4),
             )
 
         def quantise(b, grouped):
@@ -68,10 +69,29 @@ def tile_picked_phput_none_p_kernel(tc, x_words, x_scales, mem, w1, offs, slot, 
             nc.vector.quantize_mx(out=codes[:].bitcast(FP8X4), scales=plane[:], in_=grouped)
             return codes, plane
 
-        grouped0 = window0[:, STAGE:U].bitcast(BF16)
-        cast(grouped0, w_raw0)
-        weights = [quantise(0, grouped0)]
+        def product(b, h):
+            acc = psum.tile([P, HALF], F32, name="acc%d%d" % (b, h))
+            nc.tensor.matmul_mx(
+                out=acc[:],
+                lhsT=weights[b][0][:].bitcast(FP8X4),
+                lhsT_scale=weights[b][1][:],
+                rhs=picked[h][:].bitcast(FP8X4),
+                rhs_scale=x_plane[:, h * HALF : (h + 1) * HALF],
+                start=True,
+                stop=True,
+            )
+            return acc
+
+        grouped0 = laid.tile([P, P * PACK], BF16, name="grouped0", align_bytes=64, offset=2432)
+        for half in range(2):
+            cast(grouped0[:, half * HALF : (half + 1) * HALF], w_raw0[:, :, half * 64 : (half + 1) * 64])
         nc.sync.dma_start(window0[:, EARLY:U], mem[0:P, EARLY:U])
+        weights = [quantise(0, grouped0[:])]
+        shared = laid.tile([P, PACK * P + HALF - LATE], F32, name="shared", align_bytes=64, offset=0)
+        w_raw1 = shared[:, 0 : PACK * P].rearrange("p (j n) -> p j n", j=PACK)
+        nc.sync.dma_start(w_raw1, w_rows[:, :, P : 2 * P])
+        window1 = laid.tile([P, U], F32, name="window1", align_bytes=64, offset=2944)
+        nc.sync.dma_start(window1[:], mem[P : 2 * P, :])
 
         picked = []
         for h in range(2):
@@ -80,32 +100,25 @@ def tile_picked_phput_none_p_kernel(tc, x_words, x_scales, mem, w1, offs, slot, 
             nc.vector.tensor_copy(picked_words[:], word_table[:].bitcast(U32).indirect(entries))
             picked.append(picked_words)
 
+        y00 = keep.tile([P, HALF], F32, name="y00")
+        nc.scalar.copy(y00[:], product(0, 0)[:])
+        nc.vector.tensor_copy(window0[:].indirect(slot_sb[:, 0 : HALF // 16]), y00[:])
+
+        y01 = shared[:, PACK * P - LATE : PACK * P - LATE + HALF]
+        acc01 = product(0, 1)
+        nc.scalar.copy(y01[:, LATE:HALF], acc01[:, LATE:HALF])
+
         grouped1 = keep.tile([P, P * PACK], BF16, name="grouped1", align_bytes=64)
         cast(grouped1[:], w_raw1)
         weights.append(quantise(1, grouped1[:]))
-        window1 = keep.tile([P, U], F32, name="window1", tag="second", align_bytes=64)
-        nc.sync.dma_start(window1[:], mem[P : 2 * P, :])
-        windows = [window0, window1]
 
-        for b in range(N // P):
-            rows = slice(b * P, (b + 1) * P)
-            y = keep.tile([P, S], F32, name="y%d" % b)
-            for h in range(2):
-                cols = slice(h * HALF, (h + 1) * HALF)
-                acc = psum.tile([P, HALF], F32, name="acc%d%d" % (b, h))
-                nc.tensor.matmul_mx(
-                    out=acc[:],
-                    lhsT=weights[b][0][:].bitcast(FP8X4),
-                    lhsT_scale=weights[b][1][:],
-                    rhs=picked[h][:].bitcast(FP8X4),
-                    rhs_scale=x_plane[:, cols],
-                    start=True,
-                    stop=True,
-                )
-                nc.scalar.copy(y[:, cols], acc[:])
-            nc.vector.tensor_copy(windows[b][:].indirect(slot_sb[:]), y[:])
-            if b == 0:
-                nc.sync.dma_start(out[rows, :], windows[b][:])
-            else:
-                nc.sync.dma_start(out[rows, 0 : U // 2], windows[b][:, 0 : U // 2])
-                nc.scalar.dma_start(out[rows, U // 2 : U], windows[b][:, U // 2 : U])
+        nc.scalar.copy(y01[:, 0:LATE], acc01[:, 0:LATE])
+        nc.vector.tensor_copy(window0[:].indirect(slot_sb[:, HALF // 16 : S // 16]), y01)
+        nc.sync.dma_start(out[0:P, :], window0[:])
+
+        y1 = keep.tile([P, S], F32, name="y1")
+        for h in range(2):
+            nc.scalar.copy(y1[:, h * HALF : (h + 1) * HALF], product(1, h)[:])
+        nc.vector.tensor_copy(window1[:].indirect(slot_sb[:]), y1[:])
+        nc.sync.dma_start(out[P : 2 * P, 0 : U // 2], window1[:, 0 : U // 2])
+        nc.scalar.dma_start(out[P : 2 * P, U // 2 : U], window1[:, U // 2 : U])

@@ -16,9 +16,15 @@ FP8X4 = mybir.dt.float8_e4m3fn_x4
 P = 128
 PACK = 4
 HALF = S // 2
+LANES = 16
+BLOCK_STEP = 8
+QUAD = 32
+RUN = 4
 STAGE = U - P * PACK
-EARLY = 1024
+EARLY = 800
 LATE = 32
+SHARED = PACK * P - LATE + HALF
+GROUPED_BYTES = 2 * PACK * P
 
 
 def tile_picked_phput_none_p_kernel(tc, x_words, x_scales, mem, w1, offs, slot, out):
@@ -28,6 +34,9 @@ def tile_picked_phput_none_p_kernel(tc, x_words, x_scales, mem, w1, offs, slot, 
         laid = ctx.enter_context(tc.tile_pool(name="laid", bufs=1))
         psum = ctx.enter_context(tc.psum_pool(name="psum", bufs=1))
 
+        def half_of(lists, h):
+            return lists[:, h * HALF // LANES : (h + 1) * HALF // LANES]
+
         scale_table = keep.tile([P, T], U8, name="scale_table", tag="table", align_bytes=64)
         nc.vector.memset(scale_table[:, 0 : T // 2].bitcast(I32), 0)
         nc.gpsimd.memset(scale_table[:, T // 2 : T].bitcast(I32), 0)
@@ -35,32 +44,37 @@ def tile_picked_phput_none_p_kernel(tc, x_words, x_scales, mem, w1, offs, slot, 
         window0 = keep.tile([P, U], F32, name="window0", align_bytes=64)
         w_rows = w1.rearrange("(p j) n -> p j n", j=PACK)
         w_raw0 = window0[:, STAGE:U].rearrange("p (j n) -> p j n", j=PACK)
-
         nc.sync.dma_start(w_raw0, w_rows[:, :, 0:P])
-        offs_sb = keep.tile([P, S // 16], U16, name="offs_sb")
+
+        offs_sb = keep.tile([P, S // LANES], U16, name="offs_sb")
         nc.sync.dma_start(offs_sb[:], offs)
-        slot_sb = keep.tile([P, S // 16], U16, name="slot_sb")
+        slot_sb = keep.tile([P, S // LANES], U16, name="slot_sb")
         nc.sync.dma_start(slot_sb[:], slot)
-        nc.sync.dma_start(scale_table[0:P:8, :].bitcast(I32), x_scales[0].bitcast(I32))
-        word_table = keep.tile([P, T], I32, name="word_table", align_bytes=64)
+        nc.sync.dma_start(scale_table[0:P:BLOCK_STEP, :].bitcast(I32), x_scales[0].bitcast(I32))
+        word_table = keep.tile([P, T], I32, name="word_table", tag="words", align_bytes=64)
         nc.sync.dma_start(word_table[:], x_words[0].rearrange("p n t -> p (n t)").bitcast(I32))
         nc.sync.dma_start(window0[:, 0:EARLY], mem[0:P, 0:EARLY])
 
-        x_plane = keep.tile([P, S], U8, name="x_plane", align_bytes=64)
-        nc.vector.memset(x_plane[:].bitcast(I32), 0)
+        x_planes = [keep.tile([P, HALF], U8, name="x_plane0", align_bytes=64)]
+        nc.vector.memset(x_planes[0][:].bitcast(I32), 0)
 
-        picked_scales = keep.tile([P, S], U8, name="picked_scales", align_bytes=64)
-        nc.vector.tensor_copy(picked_scales[:], scale_table[:].indirect(offs_sb[:]))
-        for q in range(4):
-            (nc.sync, nc.scalar)[q % 2].dma_start(
-                x_plane[32 * q : 32 * q + 4, :].bitcast(I32),
-                picked_scales[32 * q : 32 * (q + 1) : 8, :].bitcast(I32),
-            )
+        picked_scales = []
+        for h in range(2):
+            picked_bytes = keep.tile([P, HALF], U8, name="picked_scales%d" % h, align_bytes=64)
+            nc.vector.tensor_copy(picked_bytes[:], scale_table[:].indirect(half_of(offs_sb, h)))
+            picked_scales.append(picked_bytes)
+
+        def move(h, queues):
+            for q in range(P // QUAD):
+                queues[q % len(queues)].dma_start(
+                    x_planes[h][QUAD * q : QUAD * q + QUAD // BLOCK_STEP, :].bitcast(I32),
+                    picked_scales[h][QUAD * q : QUAD * (q + 1) : BLOCK_STEP, :].bitcast(I32),
+                )
 
         def cast(grouped, raw):
             nc.scalar.copy(
-                grouped.rearrange("p (c i j) -> p c j i", i=4, j=PACK),
-                raw.rearrange("p j (c i) -> p c j i", i=4),
+                grouped.rearrange("p (c i j) -> p c j i", i=RUN, j=PACK),
+                raw.rearrange("p j (c i) -> p c j i", i=RUN),
             )
 
         def quantise(b, grouped):
@@ -69,43 +83,50 @@ def tile_picked_phput_none_p_kernel(tc, x_words, x_scales, mem, w1, offs, slot, 
             nc.vector.quantize_mx(out=codes[:].bitcast(FP8X4), scales=plane[:], in_=grouped)
             return codes, plane
 
-        def product(b, h):
-            acc = psum.tile([P, HALF], F32, name="acc%d%d" % (b, h))
+        def product(b, h, bank):
+            acc = psum.tile([P, HALF], F32, name="acc%d%d" % (b, h), tag=bank)
             nc.tensor.matmul_mx(
                 out=acc[:],
                 lhsT=weights[b][0][:].bitcast(FP8X4),
                 lhsT_scale=weights[b][1][:],
-                rhs=picked[h][:].bitcast(FP8X4),
-                rhs_scale=x_plane[:, h * HALF : (h + 1) * HALF],
+                rhs=picked_words[h][:].bitcast(FP8X4),
+                rhs_scale=x_planes[h][:],
                 start=True,
                 stop=True,
             )
             return acc
 
-        grouped0 = laid.tile([P, P * PACK], BF16, name="grouped0", align_bytes=64, offset=2432)
-        for half in range(2):
-            cast(grouped0[:, half * HALF : (half + 1) * HALF], w_raw0[:, :, half * 64 : (half + 1) * 64])
+        move(0, (nc.sync, nc.scalar))
+
+        grouped0 = laid.tile([P, P * PACK], BF16, name="grouped0", align_bytes=64, offset=4 * SHARED - GROUPED_BYTES // 2)
+        for part in range(2):
+            columns = slice(part * P // 2, (part + 1) * P // 2)
+            cast(grouped0[:, PACK * columns.start : PACK * columns.stop], w_raw0[:, :, columns])
         nc.sync.dma_start(window0[:, EARLY:U], mem[0:P, EARLY:U])
         weights = [quantise(0, grouped0[:])]
-        shared = laid.tile([P, PACK * P + HALF - LATE], F32, name="shared", align_bytes=64, offset=0)
+
+        shared = laid.tile([P, SHARED], F32, name="shared", align_bytes=64, offset=0)
         w_raw1 = shared[:, 0 : PACK * P].rearrange("p (j n) -> p j n", j=PACK)
         nc.sync.dma_start(w_raw1, w_rows[:, :, P : 2 * P])
-        window1 = laid.tile([P, U], F32, name="window1", align_bytes=64, offset=2944)
+        x_planes.append(laid.tile([P, HALF], U8, name="x_plane1", align_bytes=64, offset=4 * SHARED))
+        nc.vector.memset(x_planes[1][:].bitcast(I32), 0)
+        move(1, (nc.sync,))
+
+        picked_words = []
+        for h in range(2):
+            words = keep.tile([P, HALF], U32, name="picked_words%d" % h, align_bytes=64)
+            nc.vector.tensor_copy(words[:], word_table[:].bitcast(U32).indirect(half_of(offs_sb, h)))
+            picked_words.append(words)
+
+        window1 = keep.tile([P, U], F32, name="window1", tag="words", align_bytes=64)
         nc.sync.dma_start(window1[:], mem[P : 2 * P, :])
 
-        picked = []
-        for h in range(2):
-            picked_words = keep.tile([P, HALF], U32, name="picked_words%d" % h, align_bytes=64)
-            entries = offs_sb[:, h * HALF // 16 : (h + 1) * HALF // 16]
-            nc.vector.tensor_copy(picked_words[:], word_table[:].bitcast(U32).indirect(entries))
-            picked.append(picked_words)
-
         y00 = keep.tile([P, HALF], F32, name="y00")
-        nc.scalar.copy(y00[:], product(0, 0)[:])
-        nc.vector.tensor_copy(window0[:].indirect(slot_sb[:, 0 : HALF // 16]), y00[:])
+        nc.scalar.copy(y00[:], product(0, 0, "first")[:])
+        nc.vector.tensor_copy(window0[:].indirect(half_of(slot_sb, 0)), y00[:])
 
-        y01 = shared[:, PACK * P - LATE : PACK * P - LATE + HALF]
-        acc01 = product(0, 1)
+        y01 = shared[:, SHARED - HALF : SHARED]
+        acc01 = product(0, 1, "middle")
         nc.scalar.copy(y01[:, LATE:HALF], acc01[:, LATE:HALF])
 
         grouped1 = keep.tile([P, P * PACK], BF16, name="grouped1", align_bytes=64)
@@ -113,12 +134,12 @@ def tile_picked_phput_none_p_kernel(tc, x_words, x_scales, mem, w1, offs, slot, 
         weights.append(quantise(1, grouped1[:]))
 
         nc.scalar.copy(y01[:, 0:LATE], acc01[:, 0:LATE])
-        nc.vector.tensor_copy(window0[:].indirect(slot_sb[:, HALF // 16 : S // 16]), y01)
+        nc.vector.tensor_copy(window0[:].indirect(half_of(slot_sb, 1)), y01)
         nc.sync.dma_start(out[0:P, :], window0[:])
 
         y1 = keep.tile([P, S], F32, name="y1")
-        for h in range(2):
-            nc.scalar.copy(y1[:, h * HALF : (h + 1) * HALF], product(1, h)[:])
+        nc.scalar.copy(y1[:, 0:HALF], product(1, 0, "middle")[:])
+        nc.scalar.copy(y1[:, HALF:S], product(1, 1, "last")[:])
         nc.vector.tensor_copy(window1[:].indirect(slot_sb[:]), y1[:])
         nc.sync.dma_start(out[P : 2 * P, 0 : U // 2], window1[:, 0 : U // 2])
         nc.scalar.dma_start(out[P : 2 * P, U // 2 : U], window1[:, U // 2 : U])

@@ -51,7 +51,7 @@ def tile_picked_phput_none_p_kernel(tc, x_words, x_scales, mem, w1, offs, slot, 
         slot_sb = keep.tile([P, S // LANES], U16, name="slot_sb")
         nc.sync.dma_start(slot_sb[:], slot)
         nc.sync.dma_start(scale_table[0:P:BLOCK_STEP, :].bitcast(I32), x_scales[0].bitcast(I32))
-        word_table = keep.tile([P, T], I32, name="word_table", tag="words", align_bytes=64)
+        word_table = keep.tile([P, T], I32, name="word_table", align_bytes=64)
         nc.sync.dma_start(word_table[:], x_words[0].rearrange("p n t -> p (n t)").bitcast(I32))
         nc.sync.dma_start(window0[:, 0:EARLY], mem[0:P, 0:EARLY])
 
@@ -60,7 +60,7 @@ def tile_picked_phput_none_p_kernel(tc, x_words, x_scales, mem, w1, offs, slot, 
 
         picked_scales = []
         for h in range(2):
-            picked_bytes = keep.tile([P, HALF], U8, name="picked_scales%d" % h, align_bytes=64)
+            picked_bytes = keep.tile([P, HALF], U8, name="picked_scales%d" % h, tag=("moved", "picked1")[h], align_bytes=64)
             nc.vector.tensor_copy(picked_bytes[:], scale_table[:].indirect(half_of(offs_sb, h)))
             picked_scales.append(picked_bytes)
 
@@ -118,7 +118,7 @@ def tile_picked_phput_none_p_kernel(tc, x_words, x_scales, mem, w1, offs, slot, 
             nc.vector.tensor_copy(words[:], word_table[:].bitcast(U32).indirect(half_of(offs_sb, h)))
             picked_words.append(words)
 
-        window1 = keep.tile([P, U], F32, name="window1", tag="words", align_bytes=64)
+        window1 = keep.tile([P, U], F32, name="window1", tag="moved", align_bytes=64)
         nc.sync.dma_start(window1[:], mem[P : 2 * P, :])
 
         y00 = keep.tile([P, HALF], F32, name="y00")

@@ -21,9 +21,9 @@ BLOCK_STEP = 8
 QUAD = 32
 RUN = 4
 STAGE = U - P * PACK
-EARLY = 800
-LATE = 32
-SHARED = PACK * P - LATE + HALF
+EARLY = 832
+OWN = 96
+SHARED = PACK * P
 GROUPED_BYTES = 2 * PACK * P
 
 
@@ -125,15 +125,20 @@ def tile_picked_phput_none_p_kernel(tc, x_words, x_scales, mem, w1, offs, slot, 
         nc.scalar.copy(y00[:], product(0, 0, "first")[:])
         nc.vector.tensor_copy(window0[:].indirect(half_of(slot_sb, 0)), y00[:])
 
-        y01 = shared[:, SHARED - HALF : SHARED]
-        acc01 = product(0, 1, "middle")
-        nc.scalar.copy(y01[:, LATE:HALF], acc01[:, LATE:HALF])
-
         grouped1 = keep.tile([P, P * PACK], BF16, name="grouped1", align_bytes=64)
-        cast(grouped1[:], w_raw1)
+        cast(grouped1[:, 0 : PACK * OWN], w_raw1[:, :, 0:OWN])
+        nc.gpsimd.tensor_scalar(
+            grouped1[:, PACK * OWN : PACK * P].rearrange("p (c j) -> p c j", j=PACK),
+            w_raw1[:, :, OWN:P].rearrange("p j c -> p c j"),
+            1.0,
+            0.0,
+            op0=mybir.AluOpType.mult,
+            op1=mybir.AluOpType.add,
+        )
         weights.append(quantise(1, grouped1[:]))
 
-        nc.scalar.copy(y01[:, 0:LATE], acc01[:, 0:LATE])
+        y01 = shared[:, SHARED - HALF : SHARED]
+        nc.scalar.copy(y01, product(0, 1, "middle")[:])
         nc.vector.tensor_copy(window0[:].indirect(half_of(slot_sb, 1)), y01)
         nc.sync.dma_start(out[0:P, :], window0[:])
 

@@ -12,6 +12,7 @@ U32 = mybir.dt.uint32
 U16 = mybir.dt.uint16
 U8 = mybir.dt.uint8
 FP8X4 = mybir.dt.float8_e4m3fn_x4
+COPY = mybir.ActivationFunctionType.Copy
 
 P = 128
 PACK = 4
@@ -21,9 +22,8 @@ BLOCK_STEP = 8
 QUAD = 32
 RUN = 4
 STAGE = U - P * PACK
-EARLY = 832
-OWN = 96
-SHARED = PACK * P
+EARLY = 1408
+RAW_BYTES = 4 * PACK * P
 GROUPED_BYTES = 2 * PACK * P
 
 
@@ -34,8 +34,8 @@ def tile_picked_phput_none_p_kernel(tc, x_words, x_scales, mem, w1, offs, slot, 
         laid = ctx.enter_context(tc.tile_pool(name="laid", bufs=1))
         psum = ctx.enter_context(tc.psum_pool(name="psum", bufs=1))
 
-        def half_of(lists, h):
-            return lists[:, h * HALF // LANES : (h + 1) * HALF // LANES]
+        def half(h, per=1):
+            return slice(h * HALF // per, (h + 1) * HALF // per)
 
         scale_table = keep.tile([P, T], U8, name="scale_table", tag="table", align_bytes=64)
         nc.vector.memset(scale_table[:, 0 : T // 2].bitcast(I32), 0)
@@ -55,24 +55,18 @@ def tile_picked_phput_none_p_kernel(tc, x_words, x_scales, mem, w1, offs, slot, 
         nc.sync.dma_start(word_table[:], x_words[0].rearrange("p n t -> p (n t)").bitcast(I32))
         nc.sync.dma_start(window0[:, 0:EARLY], mem[0:P, 0:EARLY])
 
-        x_planes = [keep.tile([P, HALF], U8, name="x_plane0", align_bytes=64)]
-        nc.vector.memset(x_planes[0][:].bitcast(I32), 0)
+        x_plane = keep.tile([P, S], U8, name="x_plane", align_bytes=64)
+        nc.vector.memset(x_plane[:].bitcast(I32), 0)
+        picked_scales = keep.tile([P, S], U8, name="picked_scales", align_bytes=64)
+        nc.vector.tensor_copy(picked_scales[:], scale_table[:].indirect(offs_sb[:]))
+        for q in range(P // QUAD):
+            (nc.sync, nc.scalar)[q % 2].dma_start(
+                x_plane[QUAD * q : QUAD * q + QUAD // BLOCK_STEP, :].bitcast(I32),
+                picked_scales[QUAD * q : QUAD * (q + 1) : BLOCK_STEP, :].bitcast(I32),
+            )
 
-        picked_scales = []
-        for h in range(2):
-            picked_bytes = keep.tile([P, HALF], U8, name="picked_scales%d" % h, tag=("moved", "picked1")[h], align_bytes=64)
-            nc.vector.tensor_copy(picked_bytes[:], scale_table[:].indirect(half_of(offs_sb, h)))
-            picked_scales.append(picked_bytes)
-
-        def move(h, queues):
-            for q in range(P // QUAD):
-                queues[q % len(queues)].dma_start(
-                    x_planes[h][QUAD * q : QUAD * q + QUAD // BLOCK_STEP, :].bitcast(I32),
-                    picked_scales[h][QUAD * q : QUAD * (q + 1) : BLOCK_STEP, :].bitcast(I32),
-                )
-
-        def cast(grouped, raw):
-            nc.scalar.copy(
+        def interleaved(grouped, raw):
+            return (
                 grouped.rearrange("p (c i j) -> p c j i", i=RUN, j=PACK),
                 raw.rearrange("p j (c i) -> p c j i", i=RUN),
             )
@@ -83,68 +77,46 @@ def tile_picked_phput_none_p_kernel(tc, x_words, x_scales, mem, w1, offs, slot, 
             nc.vector.quantize_mx(out=codes[:].bitcast(FP8X4), scales=plane[:], in_=grouped)
             return codes, plane
 
-        def product(b, h, bank):
-            acc = psum.tile([P, HALF], F32, name="acc%d%d" % (b, h), tag=bank)
+        def product(b, h):
+            acc = psum.tile([P, HALF], F32, name="acc%d%d" % (b, h))
             nc.tensor.matmul_mx(
                 out=acc[:],
                 lhsT=weights[b][0][:].bitcast(FP8X4),
                 lhsT_scale=weights[b][1][:],
-                rhs=picked_words[h][:].bitcast(FP8X4),
-                rhs_scale=x_planes[h][:],
+                rhs=picked_words[:, half(h)].bitcast(FP8X4),
+                rhs_scale=x_plane[:, half(h)],
                 start=True,
                 stop=True,
             )
             return acc
 
-        move(0, (nc.sync, nc.scalar))
-
-        grouped0 = laid.tile([P, P * PACK], BF16, name="grouped0", align_bytes=64, offset=4 * SHARED - GROUPED_BYTES // 2)
+        grouped0 = laid.tile([P, P * PACK], BF16, name="grouped0", align_bytes=64, offset=RAW_BYTES - GROUPED_BYTES // 2)
         for part in range(2):
             columns = slice(part * P // 2, (part + 1) * P // 2)
-            cast(grouped0[:, PACK * columns.start : PACK * columns.stop], w_raw0[:, :, columns])
+            nc.scalar.copy(*interleaved(grouped0[:, PACK * columns.start : PACK * columns.stop], w_raw0[:, :, columns]))
         nc.sync.dma_start(window0[:, EARLY:U], mem[0:P, EARLY:U])
         weights = [quantise(0, grouped0[:])]
 
-        shared = laid.tile([P, SHARED], F32, name="shared", align_bytes=64, offset=0)
-        w_raw1 = shared[:, 0 : PACK * P].rearrange("p (j n) -> p j n", j=PACK)
-        nc.sync.dma_start(w_raw1, w_rows[:, :, P : 2 * P])
-        x_planes.append(laid.tile([P, HALF], U8, name="x_plane1", align_bytes=64, offset=4 * SHARED))
-        nc.vector.memset(x_planes[1][:].bitcast(I32), 0)
-        move(1, (nc.sync,))
-
-        picked_words = []
-        for h in range(2):
-            words = keep.tile([P, HALF], U32, name="picked_words%d" % h, align_bytes=64)
-            nc.vector.tensor_copy(words[:], word_table[:].bitcast(U32).indirect(half_of(offs_sb, h)))
-            picked_words.append(words)
-
-        window1 = keep.tile([P, U], F32, name="window1", tag="moved", align_bytes=64)
+        w_raw1 = laid.tile([P, PACK, P], F32, name="w_raw1", align_bytes=64, offset=0)
+        nc.sync.dma_start(w_raw1[:], w_rows[:, :, P : 2 * P])
+        window1 = laid.tile([P, U], F32, name="window1", align_bytes=64, offset=RAW_BYTES)
         nc.sync.dma_start(window1[:], mem[P : 2 * P, :])
 
-        y00 = keep.tile([P, HALF], F32, name="y00")
-        nc.scalar.copy(y00[:], product(0, 0, "first")[:])
-        nc.vector.tensor_copy(window0[:].indirect(half_of(slot_sb, 0)), y00[:])
+        picked_words = keep.tile([P, S], U32, name="picked_words", align_bytes=64)
+        nc.vector.tensor_copy(picked_words[:], word_table[:].bitcast(U32).indirect(offs_sb[:]))
 
-        grouped1 = keep.tile([P, P * PACK], BF16, name="grouped1", align_bytes=64)
-        cast(grouped1[:, 0 : PACK * OWN], w_raw1[:, :, 0:OWN])
-        nc.gpsimd.tensor_scalar(
-            grouped1[:, PACK * OWN : PACK * P].rearrange("p (c j) -> p c j", j=PACK),
-            w_raw1[:, :, OWN:P].rearrange("p j c -> p c j"),
-            1.0,
-            0.0,
-            op0=mybir.AluOpType.mult,
-            op1=mybir.AluOpType.add,
-        )
-        weights.append(quantise(1, grouped1[:]))
-
-        y01 = shared[:, SHARED - HALF : SHARED]
-        nc.scalar.copy(y01, product(0, 1, "middle")[:])
-        nc.vector.tensor_copy(window0[:].indirect(half_of(slot_sb, 1)), y01)
+        y0 = [keep.tile([P, HALF], F32, name="y0%d" % h) for h in range(2)]
+        for h in range(2):
+            nc.vector.tensor_copy(y0[h][:], product(0, h)[:])
+            nc.scalar.activation(window0[:].indirect(slot_sb[:, half(h, LANES)]), y0[h][:], COPY)
         nc.sync.dma_start(out[0:P, :], window0[:])
 
+        grouped1 = keep.tile([P, P * PACK], BF16, name="grouped1", align_bytes=64)
+        nc.vector.tensor_copy(*interleaved(grouped1[:], w_raw1[:]))
+        weights.append(quantise(1, grouped1[:]))
         y1 = keep.tile([P, S], F32, name="y1")
-        nc.scalar.copy(y1[:, 0:HALF], product(1, 0, "middle")[:])
-        nc.scalar.copy(y1[:, HALF:S], product(1, 1, "last")[:])
+        for h in range(2):
+            nc.vector.tensor_copy(y1[:, half(h)], product(1, h)[:])
         nc.vector.tensor_copy(window1[:].indirect(slot_sb[:]), y1[:])
         nc.sync.dma_start(out[P : 2 * P, 0 : U // 2], window1[:, 0 : U // 2])
         nc.scalar.dma_start(out[P : 2 * P, U // 2 : U], window1[:, U // 2 : U])

@@ -60,7 +60,7 @@ def tile_picked_phput_none_p_kernel(tc, x_words, x_scales, mem, w1, offs, slot, 
         picked_scales = keep.tile([P, S], U8, name="picked_scales", align_bytes=64)
         nc.vector.tensor_copy(picked_scales[:], scale_table[:].indirect(offs_sb[:]))
         for q in range(P // QUAD):
-            (nc.sync, nc.scalar)[q % 2].dma_start(
+            (nc.scalar if q == 0 else nc.sync).dma_start(
                 x_plane[QUAD * q : QUAD * q + QUAD // BLOCK_STEP, :].bitcast(I32),
                 picked_scales[QUAD * q : QUAD * (q + 1) : BLOCK_STEP, :].bitcast(I32),
             )
@@ -83,7 +83,7 @@ def tile_picked_phput_none_p_kernel(tc, x_words, x_scales, mem, w1, offs, slot, 
                 out=acc[:],
                 lhsT=weights[b][0][:].bitcast(FP8X4),
                 lhsT_scale=weights[b][1][:],
-                rhs=picked_words[:, half(h)].bitcast(FP8X4),
+                rhs=picked_words[h][:].bitcast(FP8X4),
                 rhs_scale=x_plane[:, half(h)],
                 start=True,
                 stop=True,
@@ -102,8 +102,11 @@ def tile_picked_phput_none_p_kernel(tc, x_words, x_scales, mem, w1, offs, slot, 
         window1 = laid.tile([P, U], F32, name="window1", align_bytes=64, offset=RAW_BYTES)
         nc.sync.dma_start(window1[:], mem[P : 2 * P, :])
 
-        picked_words = keep.tile([P, S], U32, name="picked_words", align_bytes=64)
-        nc.vector.tensor_copy(picked_words[:], word_table[:].bitcast(U32).indirect(offs_sb[:]))
+        picked_words = []
+        for h in range(2):
+            words = keep.tile([P, HALF], U32, name="picked_words%d" % h, align_bytes=64)
+            nc.vector.tensor_copy(words[:], word_table[:].bitcast(U32).indirect(offs_sb[:, half(h, LANES)]))
+            picked_words.append(words)
 
         y0 = [keep.tile([P, HALF], F32, name="y0%d" % h) for h in range(2)]
         for h in range(2):

@@ -23,6 +23,7 @@ QUAD = 32
 RUN = 4
 STAGE = U - P * PACK
 EARLY = 1408
+PIECES = ((0, 128), (128, 128), (256, 256))
 RAW_BYTES = 4 * PACK * P
 GROUPED_BYTES = 2 * PACK * P
 
@@ -77,14 +78,15 @@ def tile_picked_phput_none_p_kernel(tc, x_words, x_scales, mem, w1, offs, slot, 
             nc.vector.quantize_mx(out=codes[:].bitcast(FP8X4), scales=plane[:], in_=grouped)
             return codes, plane
 
-        def product(b, h):
-            acc = psum.tile([P, HALF], F32, name="acc%d%d" % (b, h))
+        def product(b, first, width):
+            h, start = divmod(first, HALF)
+            acc = psum.tile([P, width], F32, name="acc%d_%d" % (b, first))
             nc.tensor.matmul_mx(
                 out=acc[:],
                 lhsT=weights[b][0][:].bitcast(FP8X4),
                 lhsT_scale=weights[b][1][:],
-                rhs=picked_words[h][:].bitcast(FP8X4),
-                rhs_scale=x_plane[:, half(h)],
+                rhs=picked_words[h][:, start : start + width].bitcast(FP8X4),
+                rhs_scale=x_plane[:, first : first + width],
                 start=True,
                 stop=True,
             )
@@ -109,8 +111,10 @@ def tile_picked_phput_none_p_kernel(tc, x_words, x_scales, mem, w1, offs, slot, 
             picked_words.append(words)
 
         y0 = [keep.tile([P, HALF], F32, name="y0%d" % h) for h in range(2)]
+        for first, width in PIECES:
+            h, start = divmod(first, HALF)
+            nc.vector.tensor_copy(y0[h][:, start : start + width], product(0, first, width)[:])
         for h in range(2):
-            nc.vector.tensor_copy(y0[h][:], product(0, h)[:])
             nc.scalar.activation(window0[:].indirect(slot_sb[:, half(h, LANES)]), y0[h][:], COPY)
         nc.sync.dma_start(out[0:P, :], window0[:])
 
@@ -118,8 +122,8 @@ def tile_picked_phput_none_p_kernel(tc, x_words, x_scales, mem, w1, offs, slot, 
         nc.vector.tensor_copy(*interleaved(grouped1[:], w_raw1[:]))
         weights.append(quantise(1, grouped1[:]))
         y1 = keep.tile([P, S], F32, name="y1")
-        for h in range(2):
-            nc.vector.tensor_copy(y1[:, half(h)], product(1, h)[:])
+        for first in range(0, S, P):
+            nc.vector.tensor_copy(y1[:, first : first + P], product(1, first, P)[:])
         nc.vector.tensor_copy(window1[:].indirect(slot_sb[:]), y1[:])
         nc.sync.dma_start(out[P : 2 * P, 0 : U // 2], window1[:, 0 : U // 2])
         nc.scalar.dma_start(out[P : 2 * P, U // 2 : U], window1[:, U // 2 : U])

@@ -125,5 +125,4 @@ def tile_picked_phput_none_p_kernel(tc, x_words, x_scales, mem, w1, offs, slot, 
         for first in range(0, S, P):
             nc.vector.tensor_copy(y1[:, first : first + P], product(1, first, P)[:])
         nc.vector.tensor_copy(window1[:].indirect(slot_sb[:]), y1[:])
-        nc.sync.dma_start(out[P : 2 * P, 0 : U // 2], window1[:, 0 : U // 2])
-        nc.scalar.dma_start(out[P : 2 * P, U // 2 : U], window1[:, U // 2 : U])
+        nc.sync.dma_start(out[P : 2 * P, :], window1[:])

@@ -60,10 +60,10 @@ def tile_picked_phput_none_p_kernel(tc, x_words, x_scales, mem, w1, offs, slot, 
         nc.vector.memset(x_plane[:].bitcast(I32), 0)
         picked_scales = keep.tile([P, S], U8, name="picked_scales", align_bytes=64)
         nc.vector.tensor_copy(picked_scales[:], scale_table[:].indirect(offs_sb[:]))
-        for q in range(P // QUAD):
-            (nc.scalar if q == 0 else nc.sync).dma_start(
-                x_plane[QUAD * q : QUAD * q + QUAD // BLOCK_STEP, :].bitcast(I32),
-                picked_scales[QUAD * q : QUAD * (q + 1) : BLOCK_STEP, :].bitcast(I32),
+        for m in range(QUAD // BLOCK_STEP):
+            (nc.scalar if m == 0 else nc.sync).dma_start(
+                x_plane[m:P:QUAD, :].bitcast(I32),
+                picked_scales[BLOCK_STEP * m : P : QUAD, :].bitcast(I32),
             )
 
         def interleaved(grouped, raw):

@@ -39,8 +39,7 @@ def tile_picked_phput_none_p_kernel(tc, x_words, x_scales, mem, w1, offs, slot, 
             return slice(h * HALF // per, (h + 1) * HALF // per)
 
         scale_table = keep.tile([P, T], U8, name="scale_table", tag="table", align_bytes=64)
-        nc.vector.memset(scale_table[:, 0 : T // 2].bitcast(I32), 0)
-        nc.gpsimd.memset(scale_table[:, T // 2 : T].bitcast(I32), 0)
+        nc.vector.memset(scale_table[:].bitcast(I32), 0)
 
         window0 = keep.tile([P, U], F32, name="window0", align_bytes=64)
         w_rows = w1.rearrange("(p j) n -> p j n", j=PACK)

@@ -21,10 +21,9 @@ LANES = 16
 BLOCK_STEP = 8
 QUAD = 32
 RUN = 4
-STAGE = U - P * PACK
+STAGE = U - P * PACK // 2
 EARLY = 1408
 PIECES = ((0, 128), (128, 128), (256, 256))
-RAW_BYTES = 4 * PACK * P
 GROUPED_BYTES = 2 * PACK * P
 
 
@@ -38,13 +37,12 @@ def tile_picked_phput_none_p_kernel(tc, x_words, x_scales, mem, w1, offs, slot, 
         def half(h, per=1):
             return slice(h * HALF // per, (h + 1) * HALF // per)
 
-        scale_table = keep.tile([P, T], U8, name="scale_table", tag="table", align_bytes=64)
+        scale_table = laid.tile([P, T], U8, name="scale_table", align_bytes=64, offset=0)
         nc.vector.memset(scale_table[:].bitcast(I32), 0)
 
         window0 = keep.tile([P, U], F32, name="window0", align_bytes=64)
-        w_rows = w1.rearrange("(p j) n -> p j n", j=PACK)
-        w_raw0 = window0[:, STAGE:U].rearrange("p (j n) -> p j n", j=PACK)
-        nc.sync.dma_start(w_raw0, w_rows[:, :, 0:P])
+        w_raw = keep.tile([P, PACK, N], F32, name="w_raw", align_bytes=64)
+        nc.sync.dma_start(w_raw[:], w1.rearrange("(p j) n -> p j n", j=PACK))
 
         offs_sb = keep.tile([P, S // LANES], U16, name="offs_sb")
         nc.sync.dma_start(offs_sb[:], offs)
@@ -73,7 +71,7 @@ def tile_picked_phput_none_p_kernel(tc, x_words, x_scales, mem, w1, offs, slot, 
 
         def quantise(b, grouped):
             codes = keep.tile([P, P], U32, name="w_codes%d" % b, align_bytes=64)
-            plane = keep.tile([P, P], U8, name="w_plane%d" % b, tag=("table", "plane1")[b], align_bytes=64)
+            plane = laid.tile([P, P], U8, name="w_plane%d" % b, align_bytes=64, offset=b * P)
             nc.vector.quantize_mx(out=codes[:].bitcast(FP8X4), scales=plane[:], in_=grouped)
             return codes, plane
 
@@ -91,16 +89,15 @@ def tile_picked_phput_none_p_kernel(tc, x_words, x_scales, mem, w1, offs, slot, 
             )
             return acc
 
-        grouped0 = laid.tile([P, P * PACK], BF16, name="grouped0", align_bytes=64, offset=RAW_BYTES - GROUPED_BYTES // 2)
-        for part in range(2):
-            columns = slice(part * P // 2, (part + 1) * P // 2)
-            nc.scalar.copy(*interleaved(grouped0[:, PACK * columns.start : PACK * columns.stop], w_raw0[:, :, columns]))
+        grouped0 = window0[:, STAGE:U].bitcast(BF16)
+        nc.scalar.copy(*interleaved(grouped0, w_raw[:, :, 0:P]))
+        weights = [quantise(0, grouped0)]
         nc.sync.dma_start(window0[:, EARLY:U], mem[0:P, EARLY:U])
-        weights = [quantise(0, grouped0[:])]
 
-        w_raw1 = laid.tile([P, PACK, P], F32, name="w_raw1", align_bytes=64, offset=0)
-        nc.sync.dma_start(w_raw1[:], w_rows[:, :, P : 2 * P])
-        window1 = laid.tile([P, U], F32, name="window1", align_bytes=64, offset=RAW_BYTES)
+        grouped1 = laid.tile([P, P * PACK], BF16, name="grouped1", align_bytes=64, offset=T - GROUPED_BYTES)
+        nc.vector.tensor_copy(*interleaved(grouped1[:], w_raw[:, :, P:N]))
+        weights.append(quantise(1, grouped1[:]))
+        window1 = laid.tile([P, U], F32, name="window1", align_bytes=64, offset=T - GROUPED_BYTES)
         nc.sync.dma_start(window1[:], mem[P : 2 * P, :])
 
         picked_words = []
@@ -117,9 +114,6 @@ def tile_picked_phput_none_p_kernel(tc, x_words, x_scales, mem, w1, offs, slot, 
             nc.scalar.activation(window0[:].indirect(slot_sb[:, half(h, LANES)]), y0[h][:], COPY)
         nc.sync.dma_start(out[0:P, :], window0[:])
 
-        grouped1 = keep.tile([P, P * PACK], BF16, name="grouped1", align_bytes=64)
-        nc.vector.tensor_copy(*interleaved(grouped1[:], w_raw1[:]))
-        weights.append(quantise(1, grouped1[:]))
         y1 = keep.tile([P, S], F32, name="y1")
         for first in range(0, S, P):
             nc.vector.tensor_copy(y1[:, first : first + P], product(1, first, P)[:])

@@ -21,10 +21,8 @@ LANES = 16
 BLOCK_STEP = 8
 QUAD = 32
 RUN = 4
-STAGE = U - P * PACK // 2
-EARLY = 1408
-PIECES = ((0, 128), (128, 128), (256, 256))
-GROUPED_BYTES = 2 * PACK * P
+STAGE = U - 2 * N
+EARLY = 896
 
 
 def tile_picked_phput_none_p_kernel(tc, x_words, x_scales, mem, w1, offs, slot, out):
@@ -41,8 +39,9 @@ def tile_picked_phput_none_p_kernel(tc, x_words, x_scales, mem, w1, offs, slot, 
         nc.vector.memset(scale_table[:].bitcast(I32), 0)
 
         window0 = keep.tile([P, U], F32, name="window0", align_bytes=64)
-        w_raw = keep.tile([P, PACK, N], F32, name="w_raw", align_bytes=64)
-        nc.sync.dma_start(w_raw[:], w1.rearrange("(p j) n -> p j n", j=PACK))
+        w_rows = w1.rearrange("(p j) n -> p j n", j=PACK)
+        pair0 = window0[:, STAGE:U].rearrange("p (j n) -> p j n", j=2)
+        nc.sync.dma_start(pair0, w_rows[:, 0:2, :])
 
         offs_sb = keep.tile([P, S // LANES], U16, name="offs_sb")
         nc.sync.dma_start(offs_sb[:], offs)
@@ -51,27 +50,28 @@ def tile_picked_phput_none_p_kernel(tc, x_words, x_scales, mem, w1, offs, slot, 
         nc.sync.dma_start(scale_table[0:P:BLOCK_STEP, :].bitcast(I32), x_scales[0].bitcast(I32))
         word_table = keep.tile([P, T], I32, name="word_table", align_bytes=64)
         nc.sync.dma_start(word_table[:], x_words[0].rearrange("p n t -> p (n t)").bitcast(I32))
+        pair1 = keep.tile([P, 2, N], F32, name="pair1", align_bytes=64)
+        nc.sync.dma_start(pair1[:], w_rows[:, 2:PACK, :])
         nc.sync.dma_start(window0[:, 0:EARLY], mem[0:P, 0:EARLY])
 
         x_plane = keep.tile([P, S], U8, name="x_plane", align_bytes=64)
         nc.vector.memset(x_plane[:].bitcast(I32), 0)
+        ones = keep.tile([P, 1], F32, name="ones")
+        nc.vector.memset(ones[:], 1.0)
         picked_scales = keep.tile([P, S], U8, name="picked_scales", align_bytes=64)
         nc.vector.tensor_copy(picked_scales[:], scale_table[:].indirect(offs_sb[:]))
-        for m in range(QUAD // BLOCK_STEP):
-            (nc.scalar if m == 0 else nc.sync).dma_start(
-                x_plane[m:P:QUAD, :].bitcast(I32),
-                picked_scales[BLOCK_STEP * m : P : QUAD, :].bitcast(I32),
-            )
 
-        def interleaved(grouped, raw):
-            return (
-                grouped.rearrange("p (c i j) -> p c j i", i=RUN, j=PACK),
-                raw.rearrange("p j (c i) -> p c j i", i=RUN),
+        grouped = [keep.tile([P, P * PACK], BF16, name="grouped%d" % b, align_bytes=64) for b in range(2)]
+
+        def cast(b, first_plane, pair):
+            nc.scalar.copy(
+                grouped[b][:].rearrange("p (c i j) -> p c j i", i=RUN, j=PACK)[:, :, first_plane : first_plane + 2, :],
+                pair[:, :, b * P : (b + 1) * P].rearrange("p j (c i) -> p c j i", i=RUN),
             )
 
         def quantise(b, grouped):
             codes = keep.tile([P, P], U32, name="w_codes%d" % b, align_bytes=64)
-            plane = laid.tile([P, P], U8, name="w_plane%d" % b, align_bytes=64, offset=b * P)
+            plane = keep.tile([P, P], U8, name="w_plane%d" % b, align_bytes=64)
             nc.vector.quantize_mx(out=codes[:].bitcast(FP8X4), scales=plane[:], in_=grouped)
             return codes, plane
 
@@ -89,16 +89,18 @@ def tile_picked_phput_none_p_kernel(tc, x_words, x_scales, mem, w1, offs, slot, 
             )
             return acc
 
-        grouped0 = window0[:, STAGE:U].bitcast(BF16)
-        nc.scalar.copy(*interleaved(grouped0, w_raw[:, :, 0:P]))
-        weights = [quantise(0, grouped0)]
+        for b in range(2):
+            cast(b, 0, pair0)
+        for m in range(QUAD // BLOCK_STEP):
+            (nc.scalar if m == 0 else nc.sync).dma_start(
+                x_plane[m:P:QUAD, :].bitcast(I32),
+                picked_scales[BLOCK_STEP * m : P : QUAD, :].bitcast(I32),
+            )
         nc.sync.dma_start(window0[:, EARLY:U], mem[0:P, EARLY:U])
-
-        grouped1 = laid.tile([P, P * PACK], BF16, name="grouped1", align_bytes=64, offset=T - GROUPED_BYTES)
-        nc.vector.tensor_copy(*interleaved(grouped1[:], w_raw[:, :, P:N]))
-        weights.append(quantise(1, grouped1[:]))
-        window1 = laid.tile([P, U], F32, name="window1", align_bytes=64, offset=T - GROUPED_BYTES)
+        window1 = laid.tile([P, U], F32, name="window1", align_bytes=64, offset=0)
         nc.sync.dma_start(window1[:], mem[P : 2 * P, :])
+        for b in range(2):
+            cast(b, 2, pair1[:])
 
         picked_words = []
         for h in range(2):
@@ -106,14 +108,14 @@ def tile_picked_phput_none_p_kernel(tc, x_words, x_scales, mem, w1, offs, slot, 
             nc.vector.tensor_copy(words[:], word_table[:].bitcast(U32).indirect(offs_sb[:, half(h, LANES)]))
             picked_words.append(words)
 
-        y0 = [keep.tile([P, HALF], F32, name="y0%d" % h) for h in range(2)]
-        for first, width in PIECES:
-            h, start = divmod(first, HALF)
-            nc.vector.tensor_copy(y0[h][:, start : start + width], product(0, first, width)[:])
-        for h in range(2):
-            nc.scalar.activation(window0[:].indirect(slot_sb[:, half(h, LANES)]), y0[h][:], COPY)
+        weights = [quantise(0, grouped[0][:])]
+        y0 = keep.tile([P, S], F32, name="y0")
+        for first in range(0, S, P):
+            nc.vector.tensor_copy(y0[:, first : first + P], product(0, first, P)[:])
+        nc.scalar.activation(window0[:].indirect(slot_sb[:]), y0[:], COPY, scale=ones[:])
         nc.sync.dma_start(out[0:P, :], window0[:])
 
+        weights.append(quantise(1, grouped[1][:]))
         y1 = keep.tile([P, S], F32, name="y1")
         for first in range(0, S, P):
             nc.vector.tensor_copy(y1[:, first : first + P], product(1, first, P)[:])

@@ -112,12 +112,12 @@ def tile_picked_phput_none_p_kernel(tc, x_words, x_scales, mem, w1, offs, slot, 
         y0 = keep.tile([P, S], F32, name="y0")
         for first in range(0, S, P):
             nc.vector.tensor_copy(y0[:, first : first + P], product(0, first, P)[:])
-        nc.scalar.activation(window0[:].indirect(slot_sb[:]), y0[:], COPY, scale=ones[:])
+        nc.vector.tensor_copy(window0[:].indirect(slot_sb[:]), y0[:])
         nc.sync.dma_start(out[0:P, :], window0[:])
 
         weights.append(quantise(1, grouped[1][:]))
         y1 = keep.tile([P, S], F32, name="y1")
-        for first in range(0, S, P):
-            nc.vector.tensor_copy(y1[:, first : first + P], product(1, first, P)[:])
-        nc.vector.tensor_copy(window1[:].indirect(slot_sb[:]), y1[:])
+        for first in range(0, S, HALF):
+            nc.scalar.copy(y1[:, first : first + HALF], product(1, first, HALF)[:])
+        nc.scalar.activation(window1[:].indirect(slot_sb[:]), y1[:], COPY, scale=ones[:])
         nc.sync.dma_start(out[P : 2 * P, :], window1[:])

@@ -22,7 +22,7 @@ BLOCK_STEP = 8
 QUAD = 32
 RUN = 4
 STAGE = U - 2 * N
-EARLY = 896
+EARLY = 832
 
 
 def tile_picked_phput_none_p_kernel(tc, x_words, x_scales, mem, w1, offs, slot, out):

from contextlib import ExitStack

import concourse.mybir as mybir

K, T, S, N, U = 512, 2048, 512, 256, 2048
FLOPS = 2 * K * N * S

F32 = mybir.dt.float32
BF16 = mybir.dt.bfloat16
I32 = mybir.dt.int32
U32 = mybir.dt.uint32
U16 = mybir.dt.uint16
U8 = mybir.dt.uint8
FP8X4 = mybir.dt.float8_e4m3fn_x4
COPY = mybir.ActivationFunctionType.Copy

P = 128
PACK = 4
HALF = S // 2
LANES = 16
BLOCK_STEP = 8
QUAD = 32
RUN = 4
STAGE = U - 2 * N
EARLY = 832


def tile_picked_phput_none_p_kernel(tc, x_words, x_scales, mem, w1, offs, slot, out):
    nc = tc.nc
    with ExitStack() as ctx:
        keep = ctx.enter_context(tc.tile_pool(name="keep", bufs=1))
        laid = ctx.enter_context(tc.tile_pool(name="laid", bufs=1))
        psum = ctx.enter_context(tc.psum_pool(name="psum", bufs=1))

        def half(h, per=1):
            return slice(h * HALF // per, (h + 1) * HALF // per)

        scale_table = laid.tile([P, T], U8, name="scale_table", align_bytes=64, offset=0)
        nc.vector.memset(scale_table[:].bitcast(I32), 0)

        window0 = keep.tile([P, U], F32, name="window0", align_bytes=64)
        w_rows = w1.rearrange("(p j) n -> p j n", j=PACK)
        pair0 = window0[:, STAGE:U].rearrange("p (j n) -> p j n", j=2)
        nc.sync.dma_start(pair0, w_rows[:, 0:2, :])

        offs_sb = keep.tile([P, S // LANES], U16, name="offs_sb")
        nc.sync.dma_start(offs_sb[:], offs)
        slot_sb = keep.tile([P, S // LANES], U16, name="slot_sb")
        nc.sync.dma_start(slot_sb[:], slot)
        nc.sync.dma_start(scale_table[0:P:BLOCK_STEP, :].bitcast(I32), x_scales[0].bitcast(I32))
        word_table = keep.tile([P, T], I32, name="word_table", align_bytes=64)
        nc.sync.dma_start(word_table[:], x_words[0].rearrange("p n t -> p (n t)").bitcast(I32))
        pair1 = keep.tile([P, 2, N], F32, name="pair1", align_bytes=64)
        nc.sync.dma_start(pair1[:], w_rows[:, 2:PACK, :])
        nc.sync.dma_start(window0[:, 0:EARLY], mem[0:P, 0:EARLY])

        x_plane = keep.tile([P, S], U8, name="x_plane", align_bytes=64)
        nc.vector.memset(x_plane[:].bitcast(I32), 0)
        ones = keep.tile([P, 1], F32, name="ones")
        nc.vector.memset(ones[:], 1.0)
        picked_scales = keep.tile([P, S], U8, name="picked_scales", align_bytes=64)
        nc.vector.tensor_copy(picked_scales[:], scale_table[:].indirect(offs_sb[:]))

        grouped = [keep.tile([P, P * PACK], BF16, name="grouped%d" % b, align_bytes=64) for b in range(2)]

        def cast(b, first_plane, pair):
            nc.scalar.copy(
                grouped[b][:].rearrange("p (c i j) -> p c j i", i=RUN, j=PACK)[:, :, first_plane : first_plane + 2, :],
                pair[:, :, b * P : (b + 1) * P].rearrange("p j (c i) -> p c j i", i=RUN),
            )

        def quantise(b, grouped):
            codes = keep.tile([P, P], U32, name="w_codes%d" % b, align_bytes=64)
            plane = keep.tile([P, P], U8, name="w_plane%d" % b, align_bytes=64)
            nc.vector.quantize_mx(out=codes[:].bitcast(FP8X4), scales=plane[:], in_=grouped)
            return codes, plane

        def product(b, first, width):
            h, start = divmod(first, HALF)
            acc = psum.tile([P, width], F32, name="acc%d_%d" % (b, first))
            nc.tensor.matmul_mx(
                out=acc[:],
                lhsT=weights[b][0][:].bitcast(FP8X4),
                lhsT_scale=weights[b][1][:],
                rhs=picked_words[h][:, start : start + width].bitcast(FP8X4),
                rhs_scale=x_plane[:, first : first + width],
                start=True,
                stop=True,
            )
            return acc

        for b in range(2):
            cast(b, 0, pair0)
        for m in range(QUAD // BLOCK_STEP):
            (nc.scalar if m == 0 else nc.sync).dma_start(
                x_plane[m:P:QUAD, :].bitcast(I32),
                picked_scales[BLOCK_STEP * m : P : QUAD, :].bitcast(I32),
            )
        nc.sync.dma_start(window0[:, EARLY:U], mem[0:P, EARLY:U])
        window1 = laid.tile([P, U], F32, name="window1", align_bytes=64, offset=0)
        nc.sync.dma_start(window1[:], mem[P : 2 * P, :])
        for b in range(2):
            cast(b, 2, pair1[:])

        picked_words = []
        for h in range(2):
            words = keep.tile([P, HALF], U32, name="picked_words%d" % h, align_bytes=64)
            nc.vector.tensor_copy(words[:], word_table[:].bitcast(U32).indirect(offs_sb[:, half(h, LANES)]))
            picked_words.append(words)

        weights = [quantise(0, grouped[0][:])]
        y0 = keep.tile([P, S], F32, name="y0")
        for first in range(0, S, P):
            nc.vector.tensor_copy(y0[:, first : first + P], product(0, first, P)[:])
        nc.vector.tensor_copy(window0[:].indirect(slot_sb[:]), y0[:])
        nc.sync.dma_start(out[0:P, :], window0[:])

        weights.append(quantise(1, grouped[1][:]))
        y1 = keep.tile([P, S], F32, name="y1")
        for first in range(0, S, HALF):
            nc.scalar.copy(y1[:, first : first + HALF], product(1, first, HALF)[:])
        nc.scalar.activation(window1[:].indirect(slot_sb[:]), y1[:], COPY, scale=ones[:])
        nc.sync.dma_start(out[P : 2 * P, :], window1[:])
